import numpy as np
import ml_dtypes


def mxq(x, axis, fmt="e4m3"):
    dtype, down = {"e4m3": (ml_dtypes.float8_e4m3fn, 7), "e5m2": (ml_dtypes.float8_e5m2, 14)}[fmt]
    v = np.moveaxis(np.asarray(x, np.float32).astype(ml_dtypes.bfloat16).astype(np.float64), axis, -1)
    blocks = v.reshape(v.shape[:-1] + (-1, 32))
    amax = np.abs(blocks).max(-1, keepdims=True)
    byte = np.maximum(np.where(amax > 0, np.frexp(amax)[1] - 1 + 127, 0) - down, 1)
    scale = np.exp2(byte - 127.0)
    codes = (blocks / scale).astype(np.float32).astype(dtype).astype(np.float64)
    return np.moveaxis((codes * scale).reshape(v.shape), -1, axis)


WIDE = False


def mx_kscale(k):
    if not WIDE:
        return np.ones(k)
    levels = np.array([30, -30])
    if k % 512:
        return np.exp2(np.random.permutation(np.resize(levels, k // 32))).repeat(32)
    a = np.empty((k // 512, 16))
    for p in range(k // 512):
        a[p, :8] = np.random.permutation(np.resize(levels, 8))
        for g in range(8):
            far = levels[np.abs(levels - a[p, g]) >= 10]
            a[p, g + 8] = far[np.random.randint(len(far))]
    return np.exp2(a.ravel()).repeat(32)


BF16 = ml_dtypes.bfloat16


def bf(x):
    return np.asarray(x, np.float32).astype(BF16)


def f64(x):
    return np.asarray(x).astype(np.float64)


E2M1 = np.array([0.0, 0.5, 1.0, 1.5, 2.0, 3.0, 4.0, 6.0, -0.0, -0.5, -1.0, -1.5, -2.0, -3.0, -4.0, -6.0])


def pack_weight(w, fmt):
    k, n = w.shape
    w = f64(bf(w)).reshape(k // 32, 32, n)
    amax = np.abs(w).max(1)
    if fmt == "e4m3":
        byte = np.frexp(amax)[1] - 1 + 127 - 7
    else:
        mant, ex = np.frexp(amax / 6.0)
        byte = np.where(mant > 0.5, ex, ex - 1) + 127
    byte = np.clip(np.where(amax > 0, byte, 1), 1, 254)
    scaled = (w * np.exp2(127.0 - byte)[:, None, :]).reshape(k, n).astype(np.float32)
    by_word = np.ascontiguousarray(scaled.reshape(k // 512, 128, 4, n).transpose(0, 1, 3, 2))
    if fmt == "e4m3":
        words = by_word.astype(ml_dtypes.float8_e4m3fn).view(np.uint8)
    else:
        c = by_word.astype(ml_dtypes.float4_e2m1fn).view(np.uint8) & 0xF
        words = c[..., 0::2] | (c[..., 1::2] << 4)
    return np.ascontiguousarray(words), np.ascontiguousarray(byte.astype(np.uint8).reshape(k // 512, 16, n))


def unpack_weight(words, scales, fmt):
    g, p, n, _ = words.shape
    if fmt == "e4m3":
        vals = np.ascontiguousarray(words).view(ml_dtypes.float8_e4m3fn).astype(np.float64)
    else:
        nib = np.empty((g, p, n, 4), np.uint8)
        nib[..., 0::2] = words & 0xF
        nib[..., 1::2] = words >> 4
        vals = E2M1[nib]
    vals = vals * np.repeat(np.exp2(scales.astype(np.float64) - 127.0), 8, axis=1)[..., None]
    return vals.transpose(0, 1, 3, 2).reshape(g * 512, n)
def pack4(w):
    words, scales = pack_weight(w, "e2m1")
    return words.reshape(words.shape[0], 128, -1), scales


def unpack4(words, scales):
    return unpack_weight(words.reshape(words.shape[0], 128, -1, 2), scales, "e2m1")


T, D, S, V = 512, 1024, 1024, 2048


def setup_inputs():
    s = mx_kscale(D)
    t = mx_kscale(S)
    x = np.random.standard_normal((T, D)) * s
    wd = 0.7 * np.random.standard_normal((D, S)) / np.sqrt(D) / s[:, None]
    wd_words, wd_scales = pack4(wd)
    wf = np.random.standard_normal((D, V)) / np.sqrt(D) / s[:, None]
    prior = (1 + 0.1 * np.random.standard_normal(S)) * t
    c = np.random.standard_normal((S, V)) / np.sqrt(S) / t[:, None]
    bias = 0.3 * np.random.standard_normal(V)
    return {"x": bf(x), "wd_words": wd_words, "wd_scales": wd_scales,
            "wf": bf(wf), "prior": bf(prior), "c": bf(c), "bias": bf(bias)}


def reference(x, wd_words, wd_scales, wf, prior, c, bias):
    xq = mxq(f64(x), 1, "e4m3")
    draft = xq @ unpack4(wd_words, wd_scales)
    e = np.exp(draft) * f64(prior)
    head = xq @ mxq(f64(wf), 0, "e4m3")
    corr = mxq(e, 1, "e5m2") @ mxq(f64(c), 0, "e4m3")
    full = head + corr + f64(bias)
    return draft, full

from contextlib import ExitStack

import concourse.mybir as mybir
from concourse.masks import make_identity

T, D, S, V = 512, 1024, 1024, 2048
FLOPS = 2 * T * D * S + 2 * T * D * V + 2 * T * S * V

F32 = mybir.dt.float32
BF16 = mybir.dt.bfloat16
I32 = mybir.dt.int32
U32 = mybir.dt.uint32
U8 = mybir.dt.uint8
E4M3 = mybir.dt.float8_e4m3fn_x4
E5M2 = mybir.dt.float8_e5m2_x4
E2M1 = mybir.dt.float4_e2m1fn_x4
ACT = mybir.ActivationFunctionType
ALU = mybir.AluOpType

P = 128
W = 512


def tile_draft_logit_correction_s9_kernel(tc, x, wd_words, wd_scales, wf, prior, c, bias, draft, full):
    nc = tc.nc
    with ExitStack() as ctx:
        keep = ctx.enter_context(tc.tile_pool(name="keep", bufs=1))
        work = ctx.enter_context(tc.tile_pool(name="work", bufs=2))
        psum = ctx.enter_context(tc.psum_pool(name="psum", bufs=8))
        ctx.enter_context(tc.manual_schedule())

        warm = keep.tile([P, 1], F32)
        nc.gpsimd.memset(warm[:], 0.0)
        nc.scalar.activation(out=warm[:], in_=warm[:], func=ACT.Exp)
        ident = keep.tile([P, P], F32)
        make_identity(nc, ident[:])
        ident_b = keep.tile([P, P], BF16)
        nc.vector.tensor_copy(out=ident_b[:], in_=ident[:])
        wd_s = keep.tile([P, 2, S], U8, align_bytes=64)
        nc.vector.memset(wd_s[:].bitcast(I32), 0)

        bias_col = keep.tile([P, 16], BF16)
        nc.scalar.dma_start(out=bias_col[:], in_=bias.rearrange("(p i) -> p i", i=16))
        prior_sb = keep.tile([P, 2, 4], BF16)
        nc.scalar.dma_start(out=prior_sb[:], in_=prior.rearrange("(g p j) -> p g j", g=2, j=4))

        x_sb = []
        for i in range(4):
            x_tile = keep.tile([P, D], BF16, name=f"x_sb{i}")
            x_sb.append(x_tile)
        wd_w = keep.tile([P, 2, 2 * S], U8, align_bytes=64)
        raw = {}
        for m in ("f0", "f1", "c0", "c1"):
            for h in range(2):
                raw_tile = keep.tile([P, 4, 2 * W], BF16, name=f"raw_{m}_{h}")
                raw[m, h] = raw_tile

        def load_x(i):
            nc.sync.dma_start(out=x_sb[i][:], in_=x[P * i : P * (i + 1), :])

        def src_rows(m):
            src = wf if m[0] == "f" else c
            g = int(m[1])
            return src[512 * g : 512 * (g + 1), :].rearrange("(p j) n -> p j n", j=4)

        def load_quarter(m, q):
            nc.sync.dma_start(
                out=raw[m, q // 2][:, :, W * (q % 2) : W * (q % 2 + 1)], in_=src_rows(m)[:, :, W * q : W * (q + 1)]
            )

        def load_half(m, h):
            nc.sync.dma_start(out=raw[m, h][:], in_=src_rows(m)[:, :, 2 * W * h : 2 * W * (h + 1)])

        load_x(0)
        load_x(1)
        load_quarter("f0", 0)
        load_x(2)
        load_x(3)
        load_quarter("f1", 0)
        scales32 = wd_scales.bitcast(I32)
        for quad in range(4):
            nc.sync.dma_start(
                out=wd_s[32 * quad : 32 * quad + 4, :, :].bitcast(I32),
                in_=scales32[:, 4 * quad : 4 * quad + 4, :].rearrange("g r n -> r g n"),
            )
        nc.sync.dma_start(out=wd_w[:].bitcast(I32), in_=wd_words.bitcast(I32).rearrange("g p n -> p g n"))
        load_quarter("f0", 1)
        load_quarter("f1", 1)
        for h in range(2):
            for m in ("f0", "f1", "c0", "c1"):
                if h == 0 and m[0] == "f":
                    continue
                load_half(m, h)

        x_g = keep.tile([P, 2, T, 4], BF16, align_bytes=64)
        x_q = keep.tile([P, 2, T], U32, align_bytes=64)
        x_s = keep.tile([P, 2, T], U8, align_bytes=64)
        e_g = keep.tile([P, 2, T, 4], BF16, align_bytes=64)
        e_q = keep.tile([P, 2, T], U32, align_bytes=64)
        e_s = keep.tile([P, 2, T], U8, align_bytes=64)
        bias_bc = keep.tile([P, V], BF16)
        draft_sb = []
        for i in range(4):
            draft_tile = keep.tile([P, S], F32, name=f"draft_sb{i}")
            draft_sb.append(draft_tile)

        for h in range(2):
            bank = psum.tile([P, 8, P], BF16, name="bank")
            for i in range(8):
                nc.tensor.transpose(
                    bank[:, i, :], bias_col[:, 8 * h + i : 8 * h + i + 1].to_broadcast([P, P]), ident_b[:]
                )
            nc.scalar.copy(
                out=bias_bc[:].rearrange("q (p i) -> q p i", i=16)[:, :, 8 * h : 8 * h + 8],
                in_=bank[:].rearrange("q i p -> q p i"),
            )

        x_banks = {}

        def turn_x(i):
            bank = psum.tile([P, 4, P], F32, name="bank")
            words = x_sb[i][:].bitcast(F32)
            for g in range(2):
                for u in range(2):
                    nc.tensor.transpose(bank[:, 2 * g + u, :], words[:, 256 * g + u : 256 * (g + 1) : 2], ident[:])
            x_banks[i] = bank

        def copy_x(copy, i):
            words = x_g[:].rearrange("p g t k -> p (g t k)").bitcast(F32).rearrange("p (g t u) -> p g t u", g=2, u=2)
            copy(
                out=words[:, :, P * i : P * (i + 1), :],
                in_=x_banks[i][:].rearrange("p (g u) r -> p g r u", g=2),
            )

        def quant_x(g):
            nc.vector.quantize_mx(
                out=x_q[:, g, :].bitcast(E4M3), scales=x_s[:, g, :], in_=x_g[:, g].rearrange("p t k -> p (t k)")
            )

        grouped, codes, planes = {}, {}, {}

        def lay(m, q, cut):
            tile = work.tile([P, W, 4], BF16, name="grouped", align_bytes=64, bufs=4)
            src = raw[m, q // 2][:, :, W * (q % 2) : W * (q % 2 + 1)]
            for copy, lo, hi in ((nc.scalar.copy, 0, cut), (nc.vector.tensor_copy, cut, W)):
                copy(
                    out=tile[:, lo:hi, :].rearrange("p (c i) j -> p c j i", i=4),
                    in_=src[:, :, lo:hi].rearrange("p j (c i) -> p c j i", i=4),
                )
            grouped[m, q] = tile

        def quant(m, q):
            code = keep.tile([P, W], U32, name=f"code_{m}_{q}", align_bytes=64)
            plane = keep.tile([P, W], U8, name=f"plane_{m}_{q}", align_bytes=64)
            nc.vector.quantize_mx(
                out=code[:].bitcast(E4M3), scales=plane[:], in_=grouped[m, q][:].rearrange("p n j -> p (n j)")
            )
            codes[m, q], planes[m, q] = code, plane

        d_banks, e_rows, et_banks = {}, {}, {}

        def draft_mm(n):
            g, t = divmod(n, 4)
            bank = psum.tile([P, W], F32, name="bank")
            for k in range(2):
                nc.tensor.matmul_mx(
                    out=bank[:],
                    lhsT=x_q[:, k, P * t : P * (t + 1)].bitcast(E4M3),
                    lhsT_scale=x_s[:, k, P * t : P * (t + 1)],
                    rhs=wd_w[:, k, 2 * W * g : 2 * W * (g + 1)].bitcast(E2M1),
                    rhs_scale=wd_s[:, k, W * g : W * (g + 1)],
                    start=(k == 0),
                    stop=(k == 1),
                )
            d_banks[n] = bank

        def exp(n):
            rows = work.tile([P, 4, P], F32, name="e_rows", bufs=4)
            nc.scalar.activation(
                out=rows[:], in_=d_banks[n][:].rearrange("t (p j) -> t j p", j=4), func=ACT.Exp
            )
            e_rows[n] = rows

        def draft_out(copy, n):
            g, t = divmod(n, 4)
            copy(out=draft_sb[t][:, W * g : W * (g + 1)], in_=d_banks[n][:])
            if g == 1:
                nc.sync.dma_start(out=draft[P * t : P * (t + 1), :], in_=draft_sb[t][:])

        def turn_e(n):
            bank = psum.tile([P, 4, P], F32, name="bank")
            for j in range(4):
                nc.tensor.transpose(bank[:, j, :], e_rows[n][:, j, :], ident[:])
            et_banks[n] = bank

        def weigh_e(n):
            g, t = divmod(n, 4)
            nc.vector.tensor_tensor(
                out=e_g[:, g, P * t : P * (t + 1), :],
                in0=et_banks[n][:].rearrange("p j t -> p t j"),
                in1=prior_sb[:, g, :].unsqueeze(1).to_broadcast([P, P, 4]),
                op=ALU.mult,
            )

        def quant_e(g):
            nc.vector.quantize_mx(
                out=e_q[:, g, :].bitcast(E5M2), scales=e_s[:, g, :], in_=e_g[:, g].rearrange("p t k -> p (t k)")
            )

        acc = {}

        def full_mm(m, q):
            for t in range(4):
                if m == "f0":
                    bank = psum.tile([P, W], F32, name="bank")
                    acc[q, t] = bank
                k = int(m[1])
                cols = slice(P * t, P * (t + 1))
                if m[0] == "f":
                    lhs, lhs_s = x_q[:, k, cols].bitcast(E4M3), x_s[:, k, cols]
                else:
                    lhs, lhs_s = e_q[:, k, cols].bitcast(E5M2), e_s[:, k, cols]
                nc.tensor.matmul_mx(
                    out=acc[q, t][:],
                    lhsT=lhs,
                    lhsT_scale=lhs_s,
                    rhs=codes[m, q][:].bitcast(E4M3),
                    rhs_scale=planes[m, q][:],
                    start=(m == "f0"),
                    stop=(m == "c1"),
                )

        def full_out(q, t):
            tile = work.tile([P, W], F32, name="full_sb", bufs=6)
            nc.vector.tensor_tensor(out=tile[:], in0=acc[q, t][:], in1=bias_bc[:, W * q : W * (q + 1)], op=ALU.add)
            nc.sync.dma_start(out=full[P * t : P * (t + 1), W * q : W * (q + 1)], in_=tile[:])

        vcopy, scopy = nc.vector.tensor_copy, nc.scalar.copy
        head_cut, mid_cut, tail_cut = 256, 128, 352

        for i in range(4):
            turn_x(i)
        copy_x(vcopy, 0)
        copy_x(scopy, 1)
        lay("f0", 0, head_cut)
        copy_x(vcopy, 2)
        copy_x(scopy, 3)
        quant("f0", 0)
        quant_x(0)
        quant_x(1)
        lay("f1", 0, head_cut)
        full_mm("f0", 0)
        draft_mm(0)
        draft_mm(1)
        quant("f1", 0)
        mid = [("f0", 1), ("f1", 1), ("c0", 0), ("c1", 0)]
        for n in range(8):
            exp(n)
            if n + 2 < 8:
                draft_mm(n + 2)
            turn_e(n)
            if n % 2 == 0:
                lay(*mid[n // 2], mid_cut)
            elif n > 1:
                quant(*mid[n // 2 - 1])
            if n > 0:
                weigh_e(n - 1)
            draft_out(scopy, n)
            if n == 1:
                full_mm("f1", 0)
            if n == 5:
                quant_e(0)
        weigh_e(7)
        tail = [("c0", 1), ("c1", 1)] + [(m, q) for q in (2, 3) for m in ("f0", "f1", "c0", "c1")]
        lay(*tail[0], tail_cut)
        quant("c1", 0)
        quant_e(1)
        full_mm("c0", 0)
        full_mm("c1", 0)
        pending = [(0, t) for t in range(4)]
        outs = [1, 1, 1, 1, 2, 1, 1, 1, 1, 2]
        for k, unit in enumerate(tail):
            if k + 1 < len(tail):
                lay(*tail[k + 1], tail_cut)
            quant(*unit)
            for item in pending[: outs[k]]:
                full_out(*item)
            pending = pending[outs[k] :]
            if k == 0:
                full_mm("f0", 1)
                full_mm("f1", 1)
            full_mm(*unit)
            if unit[0] == "c1":
                pending += [(unit[1], t) for t in range(4)]
        for item in pending:
            full_out(*item)
